import numpy as np
import ml_dtypes


def mxq(x, axis, fmt="e4m3"):
    dtype, down = {"e4m3": (ml_dtypes.float8_e4m3fn, 7), "e5m2": (ml_dtypes.float8_e5m2, 14)}[fmt]
    v = np.moveaxis(np.asarray(x, np.float32).astype(ml_dtypes.bfloat16).astype(np.float64), axis, -1)
    blocks = v.reshape(v.shape[:-1] + (-1, 32))
    amax = np.abs(blocks).max(-1, keepdims=True)
    byte = np.maximum(np.where(amax > 0, np.frexp(amax)[1] - 1 + 127, 0) - down, 1)
    scale = np.exp2(byte - 127.0)
    codes = (blocks / scale).astype(np.float32).astype(dtype).astype(np.float64)
    return np.moveaxis((codes * scale).reshape(v.shape), -1, axis)


WIDE = False


def mx_kscale(k):
    if not WIDE:
        return np.ones(k)
    levels = np.array([30, -30])
    if k % 512:
        return np.exp2(np.random.permutation(np.resize(levels, k // 32))).repeat(32)
    a = np.empty((k // 512, 16))
    for p in range(k // 512):
        a[p, :8] = np.random.permutation(np.resize(levels, 8))
        for g in range(8):
            far = levels[np.abs(levels - a[p, g]) >= 10]
            a[p, g + 8] = far[np.random.randint(len(far))]
    return np.exp2(a.ravel()).repeat(32)


def f64(x):
    return np.asarray(x).astype(np.float64)


def striped(idx):
    return np.tile(np.asarray(idx).reshape(-1, 16).T, (8, 1)).astype(np.uint16)


def unstriped(offs):
    return offs[:16].T.reshape(-1).astype(np.int64)


E2M1 = np.array([0.0, 0.5, 1.0, 1.5, 2.0, 3.0, 4.0, 6.0, -0.0, -0.5, -1.0, -1.5, -2.0, -3.0, -4.0, -6.0])


def pack_weight(w, fmt):
    k, n = w.shape
    w = f64(np.asarray(w, np.float32).astype(ml_dtypes.bfloat16)).reshape(k // 32, 32, n)
    amax = np.abs(w).max(1)
    if fmt in ("e4m3", "e5m2"):
        byte = np.frexp(amax)[1] - 1 + 127 - (7 if fmt == "e4m3" else 14)
    else:
        mant, ex = np.frexp(amax / 6.0)
        byte = np.where(mant > 0.5, ex, ex - 1) + 127
    byte = np.clip(np.where(amax > 0, byte, 1), 1, 254)
    scaled = (w * np.exp2(127.0 - byte)[:, None, :]).reshape(k, n).astype(np.float32)
    by_word = np.ascontiguousarray(scaled.reshape(k // 512, 128, 4, n).transpose(0, 1, 3, 2))
    if fmt in ("e4m3", "e5m2"):
        words = by_word.astype(ml_dtypes.float8_e4m3fn if fmt == "e4m3" else ml_dtypes.float8_e5m2).view(np.uint8)
    else:
        c = by_word.astype(ml_dtypes.float4_e2m1fn).view(np.uint8) & 0xF
        words = (c[..., 0::2] | (c[..., 1::2] << 4)).reshape(k // 512, 128, 2 * n)
    return np.ascontiguousarray(words), np.ascontiguousarray(byte.astype(np.uint8).reshape(k // 512, 16, n))


def unpack_weight(words, scales, fmt):
    g, _, n = scales.shape
    words = np.ascontiguousarray(words).reshape(g, 128, n, -1)
    if fmt in ("e4m3", "e5m2"):
        vals = words.view(ml_dtypes.float8_e4m3fn if fmt == "e4m3" else ml_dtypes.float8_e5m2).astype(np.float64)
    else:
        nib = np.empty((g, 128, n, 4), np.uint8)
        nib[..., 0::2] = words & 0xF
        nib[..., 1::2] = words >> 4
        vals = E2M1[nib]
    vals = vals * np.repeat(np.exp2(scales.astype(np.float64) - 127.0), 8, axis=1)[..., None]
    return vals.transpose(0, 1, 3, 2).reshape(g * 512, n)


def sigmoid(v):
    return 1.0 / (1.0 + np.exp(-v))


def e4m3fn_bytes(y):
    return np.clip(np.asarray(y, np.float64), -448.0, 448.0).astype(np.float32).astype(ml_dtypes.float8_e4m3fn).view(np.uint8)


def e4m3fn_values(b):
    return np.asarray(b, np.uint8).view(ml_dtypes.float8_e4m3fn).astype(np.float64)


def sgn(shape):
    return np.random.uniform(0.5, 2.0, shape) * np.where(np.random.standard_normal(shape) < 0, -1.0, 1.0)


K, T, J, R, V, N, E = 512, 1024, 256, 512, 1024, 256, 512


def setup_inputs():
    n = np.random.standard_normal
    idx = np.random.permutation(T)[:J]
    idx2 = np.random.permutation(V)[:J]
    idx3 = np.random.permutation(E)[:J]
    fk = mx_kscale(K)
    fr = mx_kscale(R)
    xtp = pack_weight(n((K, T)) / fk[:, None], "e5m2")
    wp = pack_weight(n((K, R)) * 1 / np.sqrt(K) * fk[:, None] * fr, "e2m1")
    w2p = pack_weight(n((K, R)) * 1 / np.sqrt(K) * fk[:, None] * fr, "e4m3")
    wbp = pack_weight(n((R, N)) * 1 / np.sqrt(R) / fr[:, None], "e2m1")
    return {
        "xt_words": xtp[0],
        "xt_scales": xtp[1],
        "w_words": wp[0],
        "w_scales": wp[1],
        "w2_words": w2p[0],
        "w2_scales": w2p[1],
        "ca": e4m3fn_bytes(60.0 * n((R, V))),
        "st": (np.random.uniform(0.015, 0.045, (R, 1))).astype(np.float32),
        "wb_words": wbp[0],
        "wb_scales": wbp[1],
        "so": (sgn((N, 1))).astype(np.float32),
        "offs": striped(idx),
        "offs2": striped(idx2),
        "offs3": striped(idx3),
    }


def reference(xt_words, xt_scales, w_words, w_scales, w2_words, w2_scales, ca, st, wb_words, wb_scales, so, offs, offs2, offs3):
    idx = unstriped(offs)
    idx2 = unstriped(offs2)
    idx3 = unstriped(offs3)
    xtu = unpack_weight(xt_words, xt_scales, "e5m2")
    wu = unpack_weight(w_words, w_scales, "e2m1")
    w2u = unpack_weight(w2_words, w2_scales, "e4m3")
    wbu = unpack_weight(wb_words, wb_scales, "e2m1")
    xtidxg = xtu[:, idx]
    a = wu.T @ xtidxg
    b = w2u.T @ xtidxg
    g1 = sigmoid(e4m3fn_values(ca)[:, idx2] * f64(st))
    hid = b + g1 * (a - b)
    hidq = mxq(hid, 0, "e4m3")
    p = wbu.T @ hidq
    y = np.zeros((N, E))
    y[:, idx3] = p * f64(so)
    return y

@@ -1,0 +1,155 @@
+from contextlib import ExitStack
+
+import concourse.mybir as mybir
+
+K, T, J, R, V, N, E = 512, 1024, 256, 512, 1024, 256, 512
+FLOPS = 2 * (2 * K * R * J) + 2 * R * N * J
+
+F32 = mybir.dt.float32
+BF16 = mybir.dt.bfloat16
+I32 = mybir.dt.int32
+U32 = mybir.dt.uint32
+U16 = mybir.dt.uint16
+U8 = mybir.dt.uint8
+FP8 = mybir.dt.float8_e4m3fn
+E4M3 = mybir.dt.float8_e4m3fn_x4
+E5M2 = mybir.dt.float8_e5m2_x4
+E2M1 = mybir.dt.float4_e2m1fn_x4
+ACT = mybir.ActivationFunctionType
+ALU = mybir.AluOpType
+
+P = 128
+PACK = 4
+HALF = J // 2
+LIST_HALF = HALF // 16
+
+
+def load_scale_rows(queue, plane, scales):
+    for q in range(4):
+        queue.dma_start(out=plane[32 * q : 32 * q + 4, :].bitcast(I32), in_=scales[0, 4 * q : 4 * q + 4, :].bitcast(I32))
+
+
+def tile_list_softchoice_kernel(tc, xt_words, xt_scales, w_words, w_scales, w2_words, w2_scales, ca, st,
+                                    wb_words, wb_scales, so, offs, offs2, offs3, out):
+    nc = tc.nc
+    with ExitStack() as ctx:
+        sb = ctx.enter_context(tc.tile_pool(name="sb", bufs=1))
+        ps = ctx.enter_context(tc.psum_pool(name="ps", bufs=1))
+
+        token_list = sb.tile([P, J // 16], U16, name="token_list")
+        entry_list = sb.tile([P, J // 16], U16, name="entry_list")
+        column_list = sb.tile([P, J // 16], U16, name="column_list")
+        x_words = sb.tile([P, T], I32, name="x_words", align_bytes=64)
+        x_plane = sb.tile([P, T], U8, name="x_plane", align_bytes=64)
+        w_raw = sb.tile([P, R], U16, name="w_raw", align_bytes=64)
+        w_raw_plane = sb.tile([P, R], U8, name="w_raw_plane", align_bytes=64)
+        w2_raw = sb.tile([P, R], I32, name="w2_raw", align_bytes=64)
+        w2_raw_plane = sb.tile([P, R], U8, name="w2_raw_plane", align_bytes=64)
+        wb = sb.tile([P, N], U16, name="wb", align_bytes=64)
+        wb_plane = sb.tile([P, N], U8, name="wb_plane", align_bytes=64)
+        store_rows = [sb.tile([P, V], U8, name="store_rows%d" % t, align_bytes=64) for t in range(PACK)]
+        steps = sb.tile([P, PACK], F32, name="steps")
+        out_weights = sb.tile([P, 2], F32, name="out_weights")
+        pages = [sb.tile([P, E], F32, name="page%d" % h, align_bytes=64) for h in range(2)]
+
+        for plane in (x_plane, w_raw_plane, w2_raw_plane, wb_plane):
+            nc.vector.memset(plane[:].bitcast(I32), 0)
+        for page in pages:
+            nc.vector.memset(page[:], 0.0)
+
+        nc.sync.dma_start(entry_list[:], offs2)
+        ca_rows = ca.rearrange("(p t) v -> p t v", t=PACK)
+        for t in range(PACK):
+            nc.sync.dma_start(out=store_rows[t][:], in_=ca_rows[:, t, :])
+        nc.sync.dma_start(out=steps[:], in_=st.rearrange("(p t) o -> p (t o)", t=PACK))
+        nc.sync.dma_start(token_list[:], offs)
+        nc.sync.dma_start(out=x_words[:], in_=xt_words[0].rearrange("p n t -> p (n t)").bitcast(I32))
+        load_scale_rows(nc.sync, x_plane, xt_scales)
+        nc.sync.dma_start(out=w_raw[:].bitcast(I32), in_=w_words[0].bitcast(I32))
+        load_scale_rows(nc.sync, w_raw_plane, w_scales)
+        nc.sync.dma_start(out=w2_raw[:], in_=w2_words[0].rearrange("p n t -> p (n t)").bitcast(I32))
+        load_scale_rows(nc.sync, w2_raw_plane, w2_scales)
+        nc.sync.dma_start(out=wb[:].bitcast(I32), in_=wb_words[0].bitcast(I32))
+        load_scale_rows(nc.sync, wb_plane, wb_scales)
+        nc.sync.dma_start(column_list[:], offs3)
+        with nc.allow_non_contiguous_dma(reason="one weight for each partition and page"):
+            nc.sync.dma_start(out=out_weights[:], in_=so.rearrange("(h p) o -> p (h o)", p=P))
+
+        picked = sb.tile([P, PACK, J], U8, name="picked", align_bytes=64)
+        logits = sb.tile([P, PACK, J], F32, name="logits", align_bytes=64)
+        for t in range(PACK):
+            nc.vector.tensor_copy(out=picked[:, t, :], in_=store_rows[t][:].indirect(entry_list[:]))
+            nc.scalar.activation(out=logits[:, t, :], in_=picked[:, t, :].bitcast(FP8), func=ACT.Copy, scale=steps[:, t : t + 1])
+        gates = [sb.tile([P, HALF, PACK], F32, name="gate%d" % h, align_bytes=64) for h in range(2)]
+
+        xg_words = sb.tile([P, J], U32, name="xg_words", align_bytes=64)
+        xg_plane = sb.tile([P, J], U8, name="xg_plane", align_bytes=64)
+        nc.vector.tensor_copy(out=xg_words[:], in_=x_words[:].bitcast(U32).indirect(token_list[:]))
+        nc.vector.tensor_copy(out=xg_plane[:], in_=x_plane[:].indirect(token_list[:]))
+
+        w_dealt = sb.tile([P, R], U16, name="w_dealt", align_bytes=64)
+        w2_dealt = sb.tile([P, R], U32, name="w2_dealt", align_bytes=64)
+        w_plane = sb.tile([P, R], U8, name="w_plane", align_bytes=64)
+        w2_plane = sb.tile([P, R], U8, name="w2_plane", align_bytes=64)
+        nc.scalar.copy(out=w_dealt[:].rearrange("p (t m) -> p t m", t=PACK), in_=w_raw[:].rearrange("p (m t) -> p t m", t=PACK))
+        nc.vector.tensor_copy(out=w_plane[:].rearrange("p (t m) -> p t m", t=PACK), in_=w_raw_plane[:].rearrange("p (m t) -> p t m", t=PACK))
+        nc.scalar.activation(out=gates[0][:], in_=logits[:, :, 0:HALF].rearrange("p t j -> p j t"), func=ACT.Sigmoid)
+        nc.scalar.copy(out=w2_dealt[:].rearrange("p (t a i) -> p a t i", t=PACK, i=4),
+                       in_=w2_raw[:].bitcast(U32).rearrange("p (a i t) -> p a t i", t=PACK, i=4))
+        nc.vector.tensor_copy(out=w2_plane[:].rearrange("p (t m) -> p t m", t=PACK), in_=w2_raw_plane[:].rearrange("p (m t) -> p t m", t=PACK))
+        nc.scalar.activation(out=gates[1][:], in_=logits[:, :, HALF:J].rearrange("p t j -> p j t"), func=ACT.Sigmoid)
+
+        first = [ps.tile([P, PACK, HALF], F32, name="first%d" % h) for h in range(2)]
+        second = [ps.tile([P, PACK, HALF], F32, name="second%d" % h) for h in range(2)]
+        for h in range(2):
+            slots = slice(h * HALF, (h + 1) * HALF)
+            for bank, words, fmt, plane in ((first[h], w_dealt, E2M1, w_plane), (second[h], w2_dealt, E4M3, w2_plane)):
+                for t in range(PACK):
+                    cols = slice(t * P, (t + 1) * P)
+                    nc.tensor.matmul_mx(out=bank[:, t, :], lhsT=words[:, cols].bitcast(fmt), lhsT_scale=plane[:, cols],
+                                        rhs=xg_words[:, slots].bitcast(E5M2), rhs_scale=xg_plane[:, slots], start=True, stop=True)
+
+        share1 = [sb.tile([P, HALF, PACK], F32, name="share1_%d" % h, align_bytes=64) for h in range(2)]
+        share2 = [sb.tile([P, HALF, PACK], F32, name="share2_%d" % h, align_bytes=64) for h in range(2)]
+        hid = [sb.tile([P, HALF, PACK], BF16, name="hid%d" % h, align_bytes=64) for h in range(2)]
+        hid_words = [sb.tile([P, HALF], U32, name="hid_words%d" % h, align_bytes=64) for h in range(2)]
+        hid_plane = [sb.tile([P, HALF], U8, name="hid_plane%d" % h, align_bytes=64) for h in range(2)]
+        result = [ps.tile([P, 2, HALF], F32, name="result%d" % h) for h in range(2)]
+        staged = [sb.tile([P, 2, HALF], F32, name="staged%d" % h, align_bytes=64) for h in range(2)]
+
+        def take_first(h):
+            nc.vector.tensor_tensor(out=share1[h][:], in0=first[h][:].rearrange("p t j -> p j t"), in1=gates[h][:], op=ALU.mult)
+
+        def take_second(h):
+            nc.vector.scalar_tensor_tensor(out=share2[h][:], in0=gates[h][:], scalar=1.0, in1=second[h][:].rearrange("p t j -> p j t"),
+                                           op0=ALU.subtract, op1=ALU.mult)
+
+        def blend(h):
+            nc.vector.tensor_tensor(out=hid[h][:], in0=share1[h][:], in1=share2[h][:], op=ALU.subtract)
+
+        def project(h):
+            nc.vector.quantize_mx(out=hid_words[h][:].bitcast(E4M3), scales=hid_plane[h][:], in_=hid[h][:].rearrange("p j t -> p (j t)"))
+            for n in range(2):
+                cols = slice(n * P, (n + 1) * P)
+                nc.tensor.matmul_mx(out=result[h][:, n, :], lhsT=wb[:, cols].bitcast(E2M1), lhsT_scale=wb_plane[:, cols],
+                                    rhs=hid_words[h][:].bitcast(E4M3), rhs_scale=hid_plane[h][:], start=True, stop=True)
+
+        def put(h):
+            for n in range(2):
+                nc.scalar.activation(out=pages[n][:].indirect(column_list[:, h * LIST_HALF : (h + 1) * LIST_HALF]),
+                                     in_=staged[h][:, n, :], func=ACT.Copy, scale=out_weights[:, n : n + 1])
+
+        take_first(0)
+        take_second(0)
+        take_first(1)
+        blend(0)
+        project(0)
+        take_second(1)
+        nc.scalar.copy(out=staged[0][:], in_=result[0][:])
+        put(0)
+        blend(1)
+        project(1)
+        nc.vector.tensor_copy(out=staged[1][:], in_=result[1][:])
+        put(1)
+        for n in range(2):
+            nc.sync.dma_start(out=out[n * P : (n + 1) * P, :], in_=pages[n][:])

@@ -21,11 +21,12 @@ ALU = mybir.AluOpType
 P = 128
 PACK = 4
 HALF = J // 2
+QUARTER = HALF // 2
 LIST_HALF = HALF // 16
 
 
-def load_scale_rows(queue, plane, scales):
-    for q in range(4):
+def load_scale_rows(queue, plane, scales, quadrants):
+    for q in quadrants:
         queue.dma_start(out=plane[32 * q : 32 * q + 4, :].bitcast(I32), in_=scales[0, 4 * q : 4 * q + 4, :].bitcast(I32))
 
 
@@ -42,9 +43,8 @@ def tile_list_softchoice_kernel(tc, xt_words, xt_scales, w_words, w_scales, w2_w
         x_words = sb.tile([P, T], I32, name="x_words", align_bytes=64)
         x_plane = sb.tile([P, T], U8, name="x_plane", align_bytes=64)
         w_raw = sb.tile([P, R], U16, name="w_raw", align_bytes=64)
-        w_raw_plane = sb.tile([P, R], U8, name="w_raw_plane", align_bytes=64)
+        rows2 = sb.tile([P, 2, 2 * R], U8, name="rows2", align_bytes=64)
         w2_raw = sb.tile([P, R], I32, name="w2_raw", align_bytes=64)
-        w2_raw_plane = sb.tile([P, R], U8, name="w2_raw_plane", align_bytes=64)
         wb = sb.tile([P, N], U16, name="wb", align_bytes=64)
         wb_plane = sb.tile([P, N], U8, name="wb_plane", align_bytes=64)
         store_rows = [sb.tile([P, V], U8, name="store_rows%d" % t, align_bytes=64) for t in range(PACK)]
@@ -52,58 +52,76 @@ def tile_list_softchoice_kernel(tc, xt_words, xt_scales, w_words, w_scales, w2_w
         out_weights = sb.tile([P, 2], F32, name="out_weights")
         pages = [sb.tile([P, E], F32, name="page%d" % h, align_bytes=64) for h in range(2)]
 
-        for plane in (x_plane, w_raw_plane, w2_raw_plane, wb_plane):
-            nc.vector.memset(plane[:].bitcast(I32), 0)
+        nc.vector.memset(x_plane[:].bitcast(I32), 0)
+        nc.vector.memset(rows2[0:64].rearrange("p a c -> p (a c)").bitcast(I32), 0)
+        nc.vector.memset(wb_plane[:].bitcast(I32), 0)
+        warm = sb.tile([P, 2], F32, name="warm")
+        nc.gpsimd.memset(warm[:, 0:1], 0.0)
+        nc.scalar.activation(out=warm[:, 1:2], in_=warm[:, 0:1], func=ACT.Sigmoid)
         for page in pages:
             nc.vector.memset(page[:], 0.0)
 
         nc.sync.dma_start(entry_list[:], offs2)
+        load_scale_rows(nc.gpsimd, x_plane, xt_scales, (0, 1))
         ca_rows = ca.rearrange("(p t) v -> p t v", t=PACK)
-        for t in range(PACK):
-            nc.sync.dma_start(out=store_rows[t][:], in_=ca_rows[:, t, :])
+        nc.sync.dma_start(out=store_rows[0][:], in_=ca_rows[:, 0, :])
         nc.sync.dma_start(out=steps[:], in_=st.rearrange("(p t) o -> p (t o)", t=PACK))
+        for t in range(1, PACK):
+            nc.sync.dma_start(out=store_rows[t][:], in_=ca_rows[:, t, :])
         nc.sync.dma_start(token_list[:], offs)
         nc.sync.dma_start(out=x_words[:], in_=xt_words[0].rearrange("p n t -> p (n t)").bitcast(I32))
-        load_scale_rows(nc.sync, x_plane, xt_scales)
-        nc.sync.dma_start(out=w_raw[:].bitcast(I32), in_=w_words[0].bitcast(I32))
-        load_scale_rows(nc.sync, w_raw_plane, w_scales)
         nc.sync.dma_start(out=w2_raw[:], in_=w2_words[0].rearrange("p n t -> p (n t)").bitcast(I32))
-        load_scale_rows(nc.sync, w2_raw_plane, w2_scales)
+        for m, scales in enumerate((w_scales, w2_scales)):
+            by_quadrant = scales[0].bitcast(I32).rearrange("(a b r) c -> b r a c", a=2, b=2)
+            for b in range(2):
+                nc.sync.dma_start(out=rows2[32 * b : 32 * b + 4, :, m * R : (m + 1) * R].bitcast(I32), in_=by_quadrant[b])
+        load_scale_rows(nc.sync, x_plane, xt_scales, (2, 3))
+        nc.sync.dma_start(out=w_raw[:].bitcast(I32), in_=w_words[0].bitcast(I32))
         nc.sync.dma_start(out=wb[:].bitcast(I32), in_=wb_words[0].bitcast(I32))
-        load_scale_rows(nc.sync, wb_plane, wb_scales)
+        load_scale_rows(nc.sync, wb_plane, wb_scales, range(4))
         nc.sync.dma_start(column_list[:], offs3)
         with nc.allow_non_contiguous_dma(reason="one weight for each partition and page"):
             nc.sync.dma_start(out=out_weights[:], in_=so.rearrange("(h p) o -> p (h o)", p=P))
 
         picked = sb.tile([P, PACK, J], U8, name="picked", align_bytes=64)
         logits = sb.tile([P, PACK, J], F32, name="logits", align_bytes=64)
-        for t in range(PACK):
-            nc.vector.tensor_copy(out=picked[:, t, :], in_=store_rows[t][:].indirect(entry_list[:]))
-            nc.scalar.activation(out=logits[:, t, :], in_=picked[:, t, :].bitcast(FP8), func=ACT.Copy, scale=steps[:, t : t + 1])
-        gates = [sb.tile([P, HALF, PACK], F32, name="gate%d" % h, align_bytes=64) for h in range(2)]
 
-        xg_words = sb.tile([P, J], U32, name="xg_words", align_bytes=64)
-        xg_plane = sb.tile([P, J], U8, name="xg_plane", align_bytes=64)
-        nc.vector.tensor_copy(out=xg_words[:], in_=x_words[:].bitcast(U32).indirect(token_list[:]))
-        nc.vector.tensor_copy(out=xg_plane[:], in_=x_plane[:].indirect(token_list[:]))
+        def look_up(t, lo, hi):
+            nc.vector.tensor_copy(out=picked[:, t, lo:hi], in_=store_rows[t][:].indirect(entry_list[:, lo // 16 : hi // 16]))
+            nc.scalar.activation(out=logits[:, t, lo:hi], in_=picked[:, t, lo:hi].bitcast(FP8), func=ACT.Copy, scale=steps[:, t : t + 1])
+
+        for t in range(PACK - 1):
+            look_up(t, 0, J)
+        look_up(PACK - 1, 0, HALF)
+        gates = [sb.tile([P, HALF, PACK], F32, name="gate%d" % h, align_bytes=64) for h in range(2)]
 
         w_dealt = sb.tile([P, R], U16, name="w_dealt", align_bytes=64)
         w2_dealt = sb.tile([P, R], U32, name="w2_dealt", align_bytes=64)
-        w_plane = sb.tile([P, R], U8, name="w_plane", align_bytes=64)
-        w2_plane = sb.tile([P, R], U8, name="w2_plane", align_bytes=64)
-        nc.scalar.copy(out=w_dealt[:].rearrange("p (t m) -> p t m", t=PACK), in_=w_raw[:].rearrange("p (m t) -> p t m", t=PACK))
-        nc.vector.tensor_copy(out=w_plane[:].rearrange("p (t m) -> p t m", t=PACK), in_=w_raw_plane[:].rearrange("p (m t) -> p t m", t=PACK))
-        nc.scalar.activation(out=gates[0][:], in_=logits[:, :, 0:HALF].rearrange("p t j -> p j t"), func=ACT.Sigmoid)
+        planes = [sb.tile([P, R], U8, name="plane%d" % m, align_bytes=64) for m in range(2)]
+        xg_words = sb.tile([P, J], U32, name="xg_words", align_bytes=64)
+        xg_plane = sb.tile([P, J], U8, name="xg_plane", align_bytes=64)
+
+        def deal_plane(m):
+            nc.vector.tensor_copy(out=planes[m][:].rearrange("p (t m) -> p t m", t=PACK),
+                                  in_=rows2[:, 0, m * R : (m + 1) * R].rearrange("p (m t) -> p t m", t=PACK))
+
         nc.scalar.copy(out=w2_dealt[:].rearrange("p (t a i) -> p a t i", t=PACK, i=4),
                        in_=w2_raw[:].bitcast(U32).rearrange("p (a i t) -> p a t i", t=PACK, i=4))
-        nc.vector.tensor_copy(out=w2_plane[:].rearrange("p (t m) -> p t m", t=PACK), in_=w2_raw_plane[:].rearrange("p (m t) -> p t m", t=PACK))
+        nc.scalar.activation(out=gates[0][:], in_=logits[:, :, 0:HALF].rearrange("p t j -> p j t"), func=ACT.Sigmoid)
+        nc.scalar.copy(out=w_dealt[:].rearrange("p (t m) -> p t m", t=PACK), in_=w_raw[:].rearrange("p (m t) -> p t m", t=PACK))
+        nc.vector.tensor_copy(out=xg_words[:], in_=x_words[:].bitcast(U32).indirect(token_list[:]))
+        nc.vector.tensor_copy(out=rows2[64:128, 0, :].bitcast(I32), in_=rows2[0:64, 1, :].bitcast(I32))
+        deal_plane(1)
+        nc.vector.tensor_copy(out=xg_plane[:], in_=x_plane[:].indirect(token_list[:]))
+        deal_plane(0)
+        look_up(PACK - 1, HALF, J)
         nc.scalar.activation(out=gates[1][:], in_=logits[:, :, HALF:J].rearrange("p t j -> p j t"), func=ACT.Sigmoid)
 
         first = [ps.tile([P, PACK, HALF], F32, name="first%d" % h) for h in range(2)]
         second = [ps.tile([P, PACK, HALF], F32, name="second%d" % h) for h in range(2)]
         for h in range(2):
             slots = slice(h * HALF, (h + 1) * HALF)
-            for bank, words, fmt, plane in ((first[h], w_dealt, E2M1, w_plane), (second[h], w2_dealt, E4M3, w2_plane)):
+            for bank, words, fmt, plane in ((second[h], w2_dealt, E4M3, planes[1]), (first[h], w_dealt, E2M1, planes[0])):
                 for t in range(PACK):
                     cols = slice(t * P, (t + 1) * P)
                     nc.tensor.matmul_mx(out=bank[:, t, :], lhsT=words[:, cols].bitcast(fmt), lhsT_scale=plane[:, cols],
@@ -114,42 +132,34 @@ def tile_list_softchoice_kernel(tc, xt_words, xt_scales, w_words, w_scales, w2_w
         hid = [sb.tile([P, HALF, PACK], BF16, name="hid%d" % h, align_bytes=64) for h in range(2)]
         hid_words = [sb.tile([P, HALF], U32, name="hid_words%d" % h, align_bytes=64) for h in range(2)]
         hid_plane = [sb.tile([P, HALF], U8, name="hid_plane%d" % h, align_bytes=64) for h in range(2)]
-        result = [ps.tile([P, 2, HALF], F32, name="result%d" % h) for h in range(2)]
-        staged = [sb.tile([P, 2, HALF], F32, name="staged%d" % h, align_bytes=64) for h in range(2)]
+        result = [[ps.tile([P, HALF], F32, name="result%d_%d" % (h, n)) for n in range(2)] for h in range(2)]
+        staged = [[sb.tile([P, HALF], F32, name="staged%d_%d" % (h, n), align_bytes=64) for n in range(2)] for h in range(2)]
 
-        def take_first(h):
-            nc.vector.tensor_tensor(out=share1[h][:], in0=first[h][:].rearrange("p t j -> p j t"), in1=gates[h][:], op=ALU.mult)
+        def shares(h, c):
+            js = slice(c * QUARTER, (c + 1) * QUARTER)
+            nc.vector.scalar_tensor_tensor(out=share2[h][:, js, :], in0=gates[h][:, js, :], scalar=1.0,
+                                           in1=second[h][:, :, js].rearrange("p t j -> p j t"), op0=ALU.subtract, op1=ALU.mult)
+            nc.vector.tensor_tensor(out=share1[h][:, js, :], in0=first[h][:, :, js].rearrange("p t j -> p j t"), in1=gates[h][:, js, :], op=ALU.mult)
 
-        def take_second(h):
-            nc.vector.scalar_tensor_tensor(out=share2[h][:], in0=gates[h][:], scalar=1.0, in1=second[h][:].rearrange("p t j -> p j t"),
-                                           op0=ALU.subtract, op1=ALU.mult)
+        def blend(h, c):
+            js = slice(c * QUARTER, (c + 1) * QUARTER)
+            nc.vector.tensor_tensor(out=hid[h][:, js, :], in0=share1[h][:, js, :], in1=share2[h][:, js, :], op=ALU.subtract)
 
-        def blend(h):
-            nc.vector.tensor_tensor(out=hid[h][:], in0=share1[h][:], in1=share2[h][:], op=ALU.subtract)
-
-        def project(h):
+        for h in range(2):
+            shares(h, 0)
+            shares(h, 1)
+            blend(h, 0)
+            blend(h, 1)
             nc.vector.quantize_mx(out=hid_words[h][:].bitcast(E4M3), scales=hid_plane[h][:], in_=hid[h][:].rearrange("p j t -> p (j t)"))
             for n in range(2):
                 cols = slice(n * P, (n + 1) * P)
-                nc.tensor.matmul_mx(out=result[h][:, n, :], lhsT=wb[:, cols].bitcast(E2M1), lhsT_scale=wb_plane[:, cols],
+                nc.tensor.matmul_mx(out=result[h][n][:], lhsT=wb[:, cols].bitcast(E2M1), lhsT_scale=wb_plane[:, cols],
                                     rhs=hid_words[h][:].bitcast(E4M3), rhs_scale=hid_plane[h][:], start=True, stop=True)
-
-        def put(h):
-            for n in range(2):
+                if h == 0 and n == 0:
+                    nc.scalar.copy(out=staged[h][n][:], in_=result[h][n][:])
+                else:
+                    nc.vector.tensor_copy(out=staged[h][n][:], in_=result[h][n][:])
                 nc.scalar.activation(out=pages[n][:].indirect(column_list[:, h * LIST_HALF : (h + 1) * LIST_HALF]),
-                                     in_=staged[h][:, n, :], func=ACT.Copy, scale=out_weights[:, n : n + 1])
-
-        take_first(0)
-        take_second(0)
-        take_first(1)
-        blend(0)
-        project(0)
-        take_second(1)
-        nc.scalar.copy(out=staged[0][:], in_=result[0][:])
-        put(0)
-        blend(1)
-        project(1)
-        nc.vector.tensor_copy(out=staged[1][:], in_=result[1][:])
-        put(1)
+                                     in_=staged[h][n][:], func=ACT.Copy, scale=out_weights[:, n : n + 1])
         for n in range(2):
             nc.sync.dma_start(out=out[n * P : (n + 1) * P, :], in_=pages[n][:])

from contextlib import ExitStack

import concourse.mybir as mybir

K, T, J, R, V, N, E = 512, 1024, 256, 512, 1024, 256, 512
FLOPS = 2 * (2 * K * R * J) + 2 * R * N * J

F32 = mybir.dt.float32
BF16 = mybir.dt.bfloat16
I32 = mybir.dt.int32
U32 = mybir.dt.uint32
U16 = mybir.dt.uint16
U8 = mybir.dt.uint8
FP8 = mybir.dt.float8_e4m3fn
E4M3 = mybir.dt.float8_e4m3fn_x4
E5M2 = mybir.dt.float8_e5m2_x4
E2M1 = mybir.dt.float4_e2m1fn_x4
ACT = mybir.ActivationFunctionType
ALU = mybir.AluOpType

P = 128
PACK = 4
HALF = J // 2
QUARTER = HALF // 2
LIST_HALF = HALF // 16


def load_scale_rows(queue, plane, scales, quadrants):
    for q in quadrants:
        queue.dma_start(out=plane[32 * q : 32 * q + 4, :].bitcast(I32), in_=scales[0, 4 * q : 4 * q + 4, :].bitcast(I32))


def tile_list_softchoice_kernel(tc, xt_words, xt_scales, w_words, w_scales, w2_words, w2_scales, ca, st,
                                    wb_words, wb_scales, so, offs, offs2, offs3, out):
    nc = tc.nc
    with ExitStack() as ctx:
        sb = ctx.enter_context(tc.tile_pool(name="sb", bufs=1))
        ps = ctx.enter_context(tc.psum_pool(name="ps", bufs=1))

        token_list = sb.tile([P, J // 16], U16, name="token_list")
        entry_list = sb.tile([P, J // 16], U16, name="entry_list")
        column_list = sb.tile([P, J // 16], U16, name="column_list")
        x_words = sb.tile([P, T], I32, name="x_words", align_bytes=64)
        x_plane = sb.tile([P, T], U8, name="x_plane", align_bytes=64)
        w_raw = sb.tile([P, R], U16, name="w_raw", align_bytes=64)
        rows2 = sb.tile([P, 2, 2 * R], U8, name="rows2", align_bytes=64)
        w2_raw = sb.tile([P, R], I32, name="w2_raw", align_bytes=64)
        wb = sb.tile([P, N], U16, name="wb", align_bytes=64)
        wb_plane = sb.tile([P, N], U8, name="wb_plane", align_bytes=64)
        store_rows = [sb.tile([P, V], U8, name="store_rows%d" % t, align_bytes=64) for t in range(PACK)]
        steps = sb.tile([P, PACK], F32, name="steps")
        out_weights = sb.tile([P, 2], F32, name="out_weights")
        pages = [sb.tile([P, E], F32, name="page%d" % h, align_bytes=64) for h in range(2)]

        nc.vector.memset(x_plane[:].bitcast(I32), 0)
        nc.vector.memset(rows2[0:64].rearrange("p a c -> p (a c)").bitcast(I32), 0)
        nc.vector.memset(wb_plane[:].bitcast(I32), 0)
        warm = sb.tile([P, 2], F32, name="warm")
        nc.gpsimd.memset(warm[:, 0:1], 0.0)
        nc.scalar.activation(out=warm[:, 1:2], in_=warm[:, 0:1], func=ACT.Sigmoid)
        for page in pages:
            nc.vector.memset(page[:], 0.0)

        nc.sync.dma_start(entry_list[:], offs2)
        load_scale_rows(nc.gpsimd, x_plane, xt_scales, (0, 1))
        ca_rows = ca.rearrange("(p t) v -> p t v", t=PACK)
        nc.sync.dma_start(out=store_rows[0][:], in_=ca_rows[:, 0, :])
        nc.sync.dma_start(out=steps[:], in_=st.rearrange("(p t) o -> p (t o)", t=PACK))
        for t in range(1, PACK):
            nc.sync.dma_start(out=store_rows[t][:], in_=ca_rows[:, t, :])
        nc.sync.dma_start(token_list[:], offs)
        nc.sync.dma_start(out=x_words[:], in_=xt_words[0].rearrange("p n t -> p (n t)").bitcast(I32))
        nc.sync.dma_start(out=w2_raw[:], in_=w2_words[0].rearrange("p n t -> p (n t)").bitcast(I32))
        for m, scales in enumerate((w_scales, w2_scales)):
            by_quadrant = scales[0].bitcast(I32).rearrange("(a b r) c -> b r a c", a=2, b=2)
            for b in range(2):
                nc.sync.dma_start(out=rows2[32 * b : 32 * b + 4, :, m * R : (m + 1) * R].bitcast(I32), in_=by_quadrant[b])
        load_scale_rows(nc.sync, x_plane, xt_scales, (2, 3))
        nc.sync.dma_start(out=w_raw[:].bitcast(I32), in_=w_words[0].bitcast(I32))
        nc.sync.dma_start(out=wb[:].bitcast(I32), in_=wb_words[0].bitcast(I32))
        load_scale_rows(nc.sync, wb_plane, wb_scales, range(4))
        nc.sync.dma_start(column_list[:], offs3)
        with nc.allow_non_contiguous_dma(reason="one weight for each partition and page"):
            nc.sync.dma_start(out=out_weights[:], in_=so.rearrange("(h p) o -> p (h o)", p=P))

        picked = sb.tile([P, PACK, J], U8, name="picked", align_bytes=64)
        logits = sb.tile([P, PACK, J], F32, name="logits", align_bytes=64)

        def look_up(t, lo, hi):
            nc.vector.tensor_copy(out=picked[:, t, lo:hi], in_=store_rows[t][:].indirect(entry_list[:, lo // 16 : hi // 16]))
            nc.scalar.activation(out=logits[:, t, lo:hi], in_=picked[:, t, lo:hi].bitcast(FP8), func=ACT.Copy, scale=steps[:, t : t + 1])

        for t in range(PACK - 1):
            look_up(t, 0, J)
        look_up(PACK - 1, 0, HALF)
        gates = [sb.tile([P, HALF, PACK], F32, name="gate%d" % h, align_bytes=64) for h in range(2)]

        w_dealt = sb.tile([P, R], U16, name="w_dealt", align_bytes=64)
        w2_dealt = sb.tile([P, R], U32, name="w2_dealt", align_bytes=64)
        planes = [sb.tile([P, R], U8, name="plane%d" % m, align_bytes=64) for m in range(2)]
        xg_words = sb.tile([P, J], U32, name="xg_words", align_bytes=64)
        xg_plane = sb.tile([P, J], U8, name="xg_plane", align_bytes=64)

        def deal_plane(m):
            nc.vector.tensor_copy(out=planes[m][:].rearrange("p (t m) -> p t m", t=PACK),
                                  in_=rows2[:, 0, m * R : (m + 1) * R].rearrange("p (m t) -> p t m", t=PACK))

        nc.scalar.copy(out=w2_dealt[:].rearrange("p (t a i) -> p a t i", t=PACK, i=4),
                       in_=w2_raw[:].bitcast(U32).rearrange("p (a i t) -> p a t i", t=PACK, i=4))
        nc.scalar.activation(out=gates[0][:], in_=logits[:, :, 0:HALF].rearrange("p t j -> p j t"), func=ACT.Sigmoid)
        nc.scalar.copy(out=w_dealt[:].rearrange("p (t m) -> p t m", t=PACK), in_=w_raw[:].rearrange("p (m t) -> p t m", t=PACK))
        nc.vector.tensor_copy(out=xg_words[:], in_=x_words[:].bitcast(U32).indirect(token_list[:]))
        nc.vector.tensor_copy(out=rows2[64:128, 0, :].bitcast(I32), in_=rows2[0:64, 1, :].bitcast(I32))
        deal_plane(1)
        nc.vector.tensor_copy(out=xg_plane[:], in_=x_plane[:].indirect(token_list[:]))
        deal_plane(0)
        look_up(PACK - 1, HALF, J)
        nc.scalar.activation(out=gates[1][:], in_=logits[:, :, HALF:J].rearrange("p t j -> p j t"), func=ACT.Sigmoid)

        first = [ps.tile([P, PACK, HALF], F32, name="first%d" % h) for h in range(2)]
        second = [ps.tile([P, PACK, HALF], F32, name="second%d" % h) for h in range(2)]
        for h in range(2):
            slots = slice(h * HALF, (h + 1) * HALF)
            for bank, words, fmt, plane in ((second[h], w2_dealt, E4M3, planes[1]), (first[h], w_dealt, E2M1, planes[0])):
                for t in range(PACK):
                    cols = slice(t * P, (t + 1) * P)
                    nc.tensor.matmul_mx(out=bank[:, t, :], lhsT=words[:, cols].bitcast(fmt), lhsT_scale=plane[:, cols],
                                        rhs=xg_words[:, slots].bitcast(E5M2), rhs_scale=xg_plane[:, slots], start=True, stop=True)

        share1 = [sb.tile([P, HALF, PACK], F32, name="share1_%d" % h, align_bytes=64) for h in range(2)]
        share2 = [sb.tile([P, HALF, PACK], F32, name="share2_%d" % h, align_bytes=64) for h in range(2)]
        hid = [sb.tile([P, HALF, PACK], BF16, name="hid%d" % h, align_bytes=64) for h in range(2)]
        hid_words = [sb.tile([P, HALF], U32, name="hid_words%d" % h, align_bytes=64) for h in range(2)]
        hid_plane = [sb.tile([P, HALF], U8, name="hid_plane%d" % h, align_bytes=64) for h in range(2)]
        result = [[ps.tile([P, HALF], F32, name="result%d_%d" % (h, n)) for n in range(2)] for h in range(2)]
        staged = [[sb.tile([P, HALF], F32, name="staged%d_%d" % (h, n), align_bytes=64) for n in range(2)] for h in range(2)]

        def shares(h, c):
            js = slice(c * QUARTER, (c + 1) * QUARTER)
            nc.vector.scalar_tensor_tensor(out=share2[h][:, js, :], in0=gates[h][:, js, :], scalar=1.0,
                                           in1=second[h][:, :, js].rearrange("p t j -> p j t"), op0=ALU.subtract, op1=ALU.mult)
            nc.vector.tensor_tensor(out=share1[h][:, js, :], in0=first[h][:, :, js].rearrange("p t j -> p j t"), in1=gates[h][:, js, :], op=ALU.mult)

        def blend(h, c):
            js = slice(c * QUARTER, (c + 1) * QUARTER)
            nc.vector.tensor_tensor(out=hid[h][:, js, :], in0=share1[h][:, js, :], in1=share2[h][:, js, :], op=ALU.subtract)

        for h in range(2):
            shares(h, 0)
            shares(h, 1)
            blend(h, 0)
            blend(h, 1)
            nc.vector.quantize_mx(out=hid_words[h][:].bitcast(E4M3), scales=hid_plane[h][:], in_=hid[h][:].rearrange("p j t -> p (j t)"))
            for n in range(2):
                cols = slice(n * P, (n + 1) * P)
                nc.tensor.matmul_mx(out=result[h][n][:], lhsT=wb[:, cols].bitcast(E2M1), lhsT_scale=wb_plane[:, cols],
                                    rhs=hid_words[h][:].bitcast(E4M3), rhs_scale=hid_plane[h][:], start=True, stop=True)
                if h == 0 and n == 0:
                    nc.scalar.copy(out=staged[h][n][:], in_=result[h][n][:])
                else:
                    nc.vector.tensor_copy(out=staged[h][n][:], in_=result[h][n][:])
                nc.scalar.activation(out=pages[n][:].indirect(column_list[:, h * LIST_HALF : (h + 1) * LIST_HALF]),
                                     in_=staged[h][n][:], func=ACT.Copy, scale=out_weights[:, n : n + 1])
        for n in range(2):
            nc.sync.dma_start(out=out[n * P : (n + 1) * P, :], in_=pages[n][:])
